import numpy as np
import ml_dtypes


def mxq(x, axis, fmt="e4m3"):
    dtype, down = {"e4m3": (ml_dtypes.float8_e4m3fn, 7), "e5m2": (ml_dtypes.float8_e5m2, 14)}[fmt]
    v = np.moveaxis(np.asarray(x, np.float32).astype(ml_dtypes.bfloat16).astype(np.float64), axis, -1)
    blocks = v.reshape(v.shape[:-1] + (-1, 32))
    amax = np.abs(blocks).max(-1, keepdims=True)
    byte = np.maximum(np.where(amax > 0, np.frexp(amax)[1] - 1 + 127, 0) - down, 1)
    scale = np.exp2(byte - 127.0)
    codes = (blocks / scale).astype(np.float32).astype(dtype).astype(np.float64)
    return np.moveaxis((codes * scale).reshape(v.shape), -1, axis)


WIDE = False


def mx_kscale(k, group=512):
    if not WIDE:
        return np.ones(k)
    levels = np.array([10, -10, 5, -5, 0])
    if group != 512:
        return np.exp2(np.random.permutation(np.resize(levels, k // group))).repeat(group)
    if k % 512:
        return np.exp2(np.random.permutation(np.resize(levels, k // 32))).repeat(32)
    a = np.empty((k // 512, 16))
    for p in range(k // 512):
        a[p, :8] = np.random.permutation(np.resize(levels, 8))
        for g in range(8):
            far = levels[np.abs(levels - a[p, g]) >= 10]
            a[p, g + 8] = far[np.random.randint(len(far))]
    return np.exp2(a.ravel()).repeat(32)


def f64(x):
    return np.asarray(x).astype(np.float64)


def striped(idx):
    return np.tile(np.asarray(idx).reshape(-1, 16).T, (8, 1)).astype(np.uint16)


def unstriped(offs):
    return offs[:16].T.reshape(-1).astype(np.int64)


H, KV, D, NQ, N = 4, 2, 256, 512, 512
CAP = 2.0


def setup_inputs():
    n = np.random.standard_normal
    s = mx_kscale(D, 0)[:, None]
    u = mx_kscale(N)
    t = np.random.uniform(0.5, 2.0, N) * u
    v = n((KV, N, 128))
    v[:, :, 127] = 1.0
    return {
        "qT": (n((H, D, NQ)) * s * (0.70 / np.sqrt(D))).astype(np.float32),
        "kT": (n((KV, D, N)) / s).astype(np.float32),
        "t": t.reshape(N, 1).astype(np.float32),
        "v": (v / t[:, None]).astype(np.float32),
        "mask": (np.arange(N)[:, None] <= np.sort(np.random.randint(N // 4, N, NQ))[None, :]).astype(np.float32),
        "og": n((H, NQ, 128)).astype(np.float32),
    }


def reference(qT, kT, t, v, mask, og):
    a = np.repeat(mxq(f64(kT), 1, "e4m3"), H // KV, 0).transpose(0, 2, 1) @ mxq(f64(qT), 1, "e4m3")
    a = CAP * np.tanh(a / CAP)
    p = np.square(np.maximum(a, 0.0))
    p = p * f64(mask)
    w = p * f64(t)
    y = mxq(w, 1, "e4m3").transpose(0, 2, 1) @ np.repeat(mxq(f64(v), 1, "e4m3"), H // KV, 0)
    y = y / (y[:, :, 127:128] + 1.0)
    y = y / (1.0 + np.exp(-f64(og)))
    return y

@@ -1,0 +1,336 @@
+from contextlib import ExitStack
+
+import concourse.mybir as mybir
+
+H, KV, D, NQ, N, E = 4, 2, 256, 512, 512, 128
+CAP = 2.0
+FLOPS = 2 * H * NQ * N * (D + E)
+
+F32 = mybir.dt.float32
+BF16 = mybir.dt.bfloat16
+I32 = mybir.dt.int32
+U8 = mybir.dt.uint8
+FP8X4 = mybir.dt.float8_e4m3fn_x4
+ACT = mybir.ActivationFunctionType
+ALU = mybir.AluOpType
+
+P = 128
+PACK = 4
+ROWS = D // PACK
+QT = 128
+TILES = NQ // QT
+HALF = N // 2
+SLOTS = HALF // PACK
+LATE = False
+
+
+def tile_rows_a_relu2_mask_cap_gate_kernel(tc, qT, kT, t, v, mask, og, out):
+    nc = tc.nc
+    q_rows = qT.rearrange("(g h) (p j) n -> g (h p) j n", h=2, j=PACK)
+    k_rows = kT.rearrange("h (p j) n -> (h p) j n", j=PACK)
+    mask_rows = mask.rearrange("(p j) n -> p j n", j=PACK)
+    og_rows = og.rearrange("h (c m) e -> c m h e", m=QT)
+    out_rows = out.rearrange("h (c m) e -> c m h e", m=QT)
+
+    units = [(0, 0), (3, 0), (0, 1), (1, 0), (2, 0), (1, 1), (2, 1), (3, 1)] + [(h, c) for c in range(2, TILES) for h in range(H)]
+    groups = [(0, 0, 4), (1, 0, 4), (2, 0, 4), (3, 0, 3), (3, 3, 4)]
+
+    with ExitStack() as ctx:
+        keep = ctx.enter_context(tc.tile_pool(name="keep", bufs=1))
+        work = ctx.enter_context(tc.tile_pool(name="work", bufs=5))
+        psum = ctx.enter_context(tc.psum_pool(name="psum", bufs=2))
+        ctx.enter_context(tc.manual_schedule())
+
+        def load(name, src, queue=nc.sync):
+            dst = keep.tile(list(src.shape), F32, name=name)
+            queue.dma_start(out=dst[:], in_=src)
+            return dst
+
+        def planes(name, width):
+            return keep.tile([P, width + width // 4], I32, name=name, align_bytes=64)
+
+        def codes(pl, width, rows, c0, n):
+            return pl[rows, c0 : c0 + n].bitcast(FP8X4)
+
+        def scales(pl, width, rows, c0, n):
+            return pl[rows, width + c0 // 4 : width + (c0 + n) // 4].bitcast(U8)
+
+        every = slice(0, P)
+
+        def quantize(pl, width, c0, src):
+            n = src.shape[1] // PACK
+            nc.vector.quantize_mx(out=codes(pl, width, every, c0, n), scales=scales(pl, width, every, c0, n), in_=src)
+
+        q_raw, m_raw, og_raw = {}, {}, {}
+
+        def load_q(g, c, n):
+            q_raw[g, c] = load("q_raw%d%d" % (g, c), q_rows[g][:, :, c * QT : (c + n) * QT])
+
+        def load_mask(c, n):
+            raw = load("m_raw%d" % c, mask_rows[:, :, c * QT : (c + n) * QT])
+            for i in range(n):
+                m_raw[c + i] = raw[:, :, i * QT : (i + 1) * QT]
+
+        def load_og(c, lo, hi, queue=nc.sync):
+            og_raw[c, lo] = load("og_raw%d%d" % (c, lo), og_rows[c][:, lo:hi, :], queue)
+
+        t_sb = load("t_sb", t.rearrange("(p j) o -> p (j o)", j=PACK), nc.scalar)
+        load_og(0, 0, 1, nc.scalar)
+        k_raw = [load("k_raw%d" % a, k_rows[:, :, a * HALF : (a + 1) * HALF]) for a in range(2)]
+        load_q(0, 0, 1)
+        load_q(1, 0, 1)
+        load_mask(0, 1)
+        load_q(0, 1, 1)
+
+        k_pl = planes("k_pl", N)
+        k_swapped = planes("k_swapped", N)
+        nc.vector.memset(k_pl[:, N : N + N // 4], 0)
+
+        t_abs = keep.tile([P, PACK], F32)
+        guess = keep.tile([P, PACK], F32)
+        t_sign = keep.tile([P, PACK], F32)
+        inverse = keep.tile([P, PACK], F32)
+        quotient = keep.tile([P, PACK], F32)
+        root = keep.tile([P, PACK], F32)
+        gate = keep.tile([P, TILES, H, E], F32)
+
+        def gates(c, lo, hi):
+            nc.scalar.activation(out=gate[:, c, lo:hi, :], in_=og_raw[c, lo][:], func=ACT.Sigmoid)
+
+        nc.vector.scalar_tensor_tensor(out=t_abs[:], in0=t_sb[:], scalar=-1.0, in1=t_sb[:], op0=ALU.mult, op1=ALU.max)
+        nc.scalar.activation(out=guess[:], in_=t_abs[:], func=ACT.Sqrt, scale=CAP * CAP)
+        nc.scalar.activation(out=t_sign[:], in_=t_sb[:], func=ACT.Sign)
+        gates(0, 0, 1)
+        nc.vector.reciprocal(out=inverse[:], in_=guess[:])
+        nc.vector.scalar_tensor_tensor(out=quotient[:], in0=inverse[:], scalar=0.5 * CAP * CAP, in1=t_abs[:], op0=ALU.mult, op1=ALU.mult)
+        nc.vector.scalar_tensor_tensor(out=root[:], in0=guess[:], scalar=0.5, in1=quotient[:], op0=ALU.mult, op1=ALU.add)
+
+        def interleave_k(a, lo, hi, copy):
+            copy(
+                out=k_bf[a][:, :, lo:hi, :].rearrange("p r s j -> p s j r"),
+                in_=k_raw[a][:, :, lo * PACK : hi * PACK].rearrange("p j (s r) -> p s j r", r=PACK),
+            )
+
+        def quantize_k(a):
+            for r in range(PACK):
+                quantize(k_pl, N, r * P + a * SLOTS, k_bf[a][:, r, :, :].rearrange("p s j -> p (s j)"))
+
+        q_bf = {}
+        q_pl = {}
+
+        def interleave_q(g, c, copy):
+            raw = q_raw[g, c]
+            qb = keep.tile([P, raw.shape[2] * PACK], BF16, name="q_bf%d%d" % (g, c), align_bytes=64)
+            copy(out=qb[:].rearrange("p (c i j) -> p c j i", i=4, j=PACK), in_=raw[:].rearrange("p j (c i) -> p c j i", i=4))
+            q_bf[g, c] = qb
+
+        def quantize_q(g, c):
+            width = q_raw[g, c].shape[2]
+            pl = planes("q_pl%d%d" % (g, c), width)
+            quantize(pl, width, 0, q_bf[g, c][:])
+            for i in range(width // QT):
+                q_pl[g, c + i] = (pl, width, i * QT)
+
+        weight = {}
+
+        def scale_mask(c):
+            ms = keep.tile([P, QT * PACK], F32, name="weight%d" % c)
+            if LATE:
+                for j in range(PACK):
+                    nc.vector.tensor_scalar(out=ms[:, j * QT : (j + 1) * QT], in0=m_raw[c][:, j, :], scalar1=root[:, j : j + 1], scalar2=None, op0=ALU.mult)
+            else:
+                nc.vector.tensor_tensor(
+                    out=ms[:].rearrange("p (c i j) -> p c j i", i=4, j=PACK),
+                    in0=m_raw[c].rearrange("p j (c i) -> p c j i", i=4),
+                    in1=root[:].unsqueeze(1).unsqueeze(3).to_broadcast([P, QT // 4, PACK, 4]),
+                    op=ALU.mult,
+                )
+            weight[c] = ms
+
+        k_bf = [keep.tile([P, PACK, SLOTS, PACK], BF16, name="k_bf%d" % a, align_bytes=64) for a in range(2)]
+        interleave_k(0, 0, SLOTS, nc.vector.tensor_copy)
+        quantize_k(0)
+        interleave_k(1, 0, 64, nc.vector.tensor_copy)
+
+        interleave_q(0, 0, nc.scalar.copy)
+        quantize_k(1)
+        quantize_q(0, 0)
+        nc.scalar.dma_start(out=k_swapped[ROWS:P, :], in_=k_pl[0:ROWS, :])
+        nc.scalar.dma_start(out=k_swapped[0:ROWS, :], in_=k_pl[ROWS:P, :])
+
+        load_mask(1, 1)
+        load_q(1, 1, 1)
+        load_q(0, 2, 2)
+        load_og(0, 1, H)
+        load_mask(2, 2)
+        load_q(1, 2, 2)
+        v_raw = load("v_raw", v.rearrange("h (p j) e -> p h (j e)", j=PACK))
+        for c in range(1, TILES):
+            load_og(c, 0, H)
+
+        v_bf = keep.tile([P, KV, E * PACK], BF16, align_bytes=64)
+        v_pl = planes("v_pl", KV * E)
+
+        def interleave_v(g):
+            nc.vector.tensor_tensor(
+                out=v_bf[:, g, :].rearrange("p (c i j) -> p c j i", i=4, j=PACK),
+                in0=v_raw[:, g, :].rearrange("p (j c i) -> p c j i", i=4, j=PACK),
+                in1=t_sign[:].unsqueeze(1).unsqueeze(3).to_broadcast([P, E // 4, PACK, 4]),
+                op=ALU.mult,
+            )
+
+        def quantize_v():
+            quantize(v_pl, KV * E, 0, v_bf[:].rearrange("p g n -> p (g n)"))
+
+        banks, capped, scaled, squared, w_pl, sums = {}, {}, {}, {}, {}, {}
+
+        def scores(u):
+            h, c = units[u]
+            rows = slice(ROWS * (h % 2), ROWS * (h % 2 + 1))
+            keys = k_pl if h // 2 == h % 2 else k_swapped
+            pl, width, c0 = q_pl[h // 2, c]
+            bank = psum.tile([P, PACK, QT], F32, name="scores%d" % (h % 2))
+            for r in range(PACK):
+                nc.tensor.matmul_mx(
+                    out=bank[:, r, :],
+                    lhsT=codes(keys, N, rows, r * P, P),
+                    lhsT_scale=scales(keys, N, rows, r * P, P),
+                    rhs=codes(pl, width, rows, c0, QT),
+                    rhs_scale=scales(pl, width, rows, c0, QT),
+                    start=True,
+                    stop=True,
+                )
+            banks[u] = bank
+
+        def cap(u):
+            th = work.tile([P, QT * PACK], F32, name="capped")
+            if LATE:
+                nc.scalar.activation(out=th[:], in_=banks[u][:].rearrange("p r q -> p (r q)"), func=ACT.Tanh, scale=1.0 / CAP)
+            else:
+                nc.scalar.activation(
+                    out=th[:].rearrange("p (q r) -> p q r", r=PACK), in_=banks[u][:].rearrange("p r q -> p q r"), func=ACT.Tanh, scale=1.0 / CAP
+                )
+            capped[u] = th
+
+        def weigh(u):
+            x = work.tile([P, QT * PACK], F32, name="scaled")
+            nc.vector.scalar_tensor_tensor(out=x[:], in0=capped[u][:], scalar=0.0, in1=weight[units[u][1]][:], op0=ALU.max, op1=ALU.mult)
+            scaled[u] = x
+
+        def square(u):
+            wb = work.tile([P, QT * PACK], BF16, name="squared", align_bytes=64)
+            if LATE:
+                nc.scalar.activation(
+                    out=wb[:].rearrange("p (c i r) -> p c r i", i=4, r=PACK),
+                    in_=scaled[u][:].rearrange("p (r c i) -> p c r i", i=4, r=PACK),
+                    func=ACT.Square,
+                )
+            else:
+                nc.scalar.activation(out=wb[:], in_=scaled[u][:], func=ACT.Square)
+            squared[u] = wb
+
+        def new_squared(u):
+            squared[u] = work.tile([P, QT * PACK], BF16, name="squared", align_bytes=64)
+            return squared[u][:]
+
+        def quantize_w(u):
+            w_pl[u] = planes("w_pl%d" % u, QT)
+            quantize(w_pl[u], QT, 0, squared[u][:])
+
+        def mix(u):
+            h, c = units[u]
+            g = [i for i, (cc, lo, hi) in enumerate(groups) if cc == c and lo <= h < hi][0]
+            if g not in sums:
+                sums[g] = psum.tile([P, H, E], F32, name="sums", bufs=4)
+            nc.tensor.matmul_mx(
+                out=sums[g][:, h, :],
+                lhsT=codes(w_pl[u], QT, every, 0, QT),
+                lhsT_scale=scales(w_pl[u], QT, every, 0, QT),
+                rhs=codes(v_pl, KV * E, every, (h // 2) * E, E),
+                rhs_scale=scales(v_pl, KV * E, every, (h // 2) * E, E),
+                start=True,
+                stop=True,
+            )
+
+        dens, recs = {}, {}
+
+        def denominators(g):
+            c, lo, hi = groups[g]
+            dens[g] = keep.tile([P, H], F32, name="den%d" % g)
+            nc.vector.tensor_scalar(out=dens[g][:, lo:hi], in0=sums[g][:, lo:hi, E - 1], scalar1=1.0, scalar2=None, op0=ALU.add)
+
+        def reciprocals(g):
+            c, lo, hi = groups[g]
+            recs[g] = keep.tile([P, H], F32, name="rec%d" % g)
+            nc.vector.reciprocal(out=recs[g][:, lo:hi], in_=dens[g][:, lo:hi])
+
+        def finish(g):
+            c, lo, hi = groups[g]
+            res = keep.tile([P, hi - lo, E], F32, name="res%d" % g)
+            for h in range(lo, hi):
+                nc.vector.scalar_tensor_tensor(
+                    out=res[:, h - lo, :],
+                    in0=sums[g][:, h, :],
+                    scalar=recs[g][:, h : h + 1],
+                    in1=gate[:, c, h, :],
+                    op0=ALU.mult,
+                    op1=ALU.mult,
+                )
+            nc.sync.dma_start(out=out_rows[c][:, lo:hi, :], in_=res[:])
+
+        vcopy = nc.vector.tensor_copy
+        extra = {
+            1: [lambda: quantize_q(0, 1), lambda: scores(2)],
+            2: [lambda: scale_mask(1)],
+            3: [lambda: interleave_q(1, 1, vcopy)],
+            4: [lambda: quantize_q(1, 1)],
+            5: [lambda: interleave_q(0, 2, vcopy), lambda: gates(0, 1, H)],
+            6: [lambda: quantize_q(0, 2), lambda: scale_mask(2)],
+            7: [lambda: interleave_q(1, 2, vcopy)],
+            8: [lambda: quantize_q(1, 2), lambda: interleave_v(0)],
+            9: [lambda: interleave_v(1), lambda: gates(1, 0, H)],
+            10: [quantize_v, lambda: scale_mask(3), lambda: gates(2, 0, H)],
+            11: [lambda: denominators(0), lambda: gates(3, 0, H)],
+            12: [lambda: reciprocals(0), lambda: denominators(1)],
+            13: [lambda: reciprocals(1), lambda: finish(0)],
+            14: [lambda: finish(1)],
+            15: [lambda: denominators(2)],
+            16: [lambda: reciprocals(2)],
+            17: [lambda: finish(2)],
+        }
+
+        scores(0)
+        interleave_q(1, 0, nc.scalar.copy)
+        quantize_q(1, 0)
+        scale_mask(0)
+        scores(1)
+        interleave_q(0, 1, vcopy)
+        count = len(units)
+        mixed = 0
+        on_vector = ()
+        for i in range(count + 2):
+            if 0 <= i - 2 < count and i - 2 not in on_vector:
+                square(i - 2)
+            if 0 <= i - 1 < count:
+                weigh(i - 1)
+            if i < count:
+                cap(i)
+            if i - 2 in on_vector:
+                nc.vector.tensor_tensor(out=new_squared(i - 2), in0=scaled[i - 2][:], in1=scaled[i - 2][:], op=ALU.mult)
+            if 0 <= i - 3 < count:
+                quantize_w(i - 3)
+            for step in extra.get(i, []):
+                step()
+            if 1 <= i and i + 2 < count:
+                scores(i + 2)
+            while i >= 10 and mixed <= i - 3:
+                mix(mixed)
+                mixed = mixed + 1
+        quantize_w(count - 1)
+        mix(count - 1)
+        denominators(3)
+        reciprocals(3)
+        denominators(4)
+        finish(3)
+        reciprocals(4)
+        finish(4)

@@ -21,7 +21,7 @@ QT = 128
 TILES = NQ // QT
 HALF = N // 2
 SLOTS = HALF // PACK
-LATE = False
+LATE = True
 
 
 def tile_rows_a_relu2_mask_cap_gate_kernel(tc, qT, kT, t, v, mask, og, out):
@@ -76,8 +76,9 @@ def tile_rows_a_relu2_mask_cap_gate_kernel(tc, qT, kT, t, v, mask, og, out):
 
         t_sb = load("t_sb", t.rearrange("(p j) o -> p (j o)", j=PACK), nc.scalar)
         load_og(0, 0, 1, nc.scalar)
-        k_raw = [load("k_raw%d" % a, k_rows[:, :, a * HALF : (a + 1) * HALF]) for a in range(2)]
+        k_raw = [load("k_raw0", k_rows[:, :, 0:HALF])]
         load_q(0, 0, 1)
+        k_raw.append(load("k_raw1", k_rows[:, :, HALF:N]))
         load_q(1, 0, 1)
         load_mask(0, 1)
         load_q(0, 1, 1)
@@ -150,11 +151,11 @@ def tile_rows_a_relu2_mask_cap_gate_kernel(tc, qT, kT, t, v, mask, og, out):
         k_bf = [keep.tile([P, PACK, SLOTS, PACK], BF16, name="k_bf%d" % a, align_bytes=64) for a in range(2)]
         interleave_k(0, 0, SLOTS, nc.vector.tensor_copy)
         quantize_k(0)
-        interleave_k(1, 0, 64, nc.vector.tensor_copy)
-
         interleave_q(0, 0, nc.scalar.copy)
-        quantize_k(1)
+        interleave_k(1, 0, 44, nc.vector.tensor_copy)
+        interleave_k(1, 44, SLOTS, nc.scalar.copy)
         quantize_q(0, 0)
+        quantize_k(1)
         nc.scalar.dma_start(out=k_swapped[ROWS:P, :], in_=k_pl[0:ROWS, :])
         nc.scalar.dma_start(out=k_swapped[0:ROWS, :], in_=k_pl[ROWS:P, :])
 
@@ -171,12 +172,15 @@ def tile_rows_a_relu2_mask_cap_gate_kernel(tc, qT, kT, t, v, mask, og, out):
         v_bf = keep.tile([P, KV, E * PACK], BF16, align_bytes=64)
         v_pl = planes("v_pl", KV * E)
 
-        def interleave_v(g):
-            nc.vector.tensor_tensor(
-                out=v_bf[:, g, :].rearrange("p (c i j) -> p c j i", i=4, j=PACK),
-                in0=v_raw[:, g, :].rearrange("p (j c i) -> p c j i", i=4, j=PACK),
-                in1=t_sign[:].unsqueeze(1).unsqueeze(3).to_broadcast([P, E // 4, PACK, 4]),
-                op=ALU.mult,
+        v_signed = keep.tile([P, KV, PACK, E], F32)
+
+        def sign_v():
+            for j in range(PACK):
+                nc.vector.tensor_scalar(out=v_signed[:, :, j, :], in0=v_raw[:, :, j * E : (j + 1) * E], scalar1=t_sign[:, j : j + 1], scalar2=None, op0=ALU.mult)
+
+        def interleave_v():
+            nc.vector.tensor_copy(
+                out=v_bf[:].rearrange("p g (c i j) -> p g c j i", i=4, j=PACK), in_=v_signed[:].rearrange("p g j (c i) -> p g c j i", i=4)
             )
 
         def quantize_v():
@@ -287,50 +291,51 @@ def tile_rows_a_relu2_mask_cap_gate_kernel(tc, qT, kT, t, v, mask, og, out):
             5: [lambda: interleave_q(0, 2, vcopy), lambda: gates(0, 1, H)],
             6: [lambda: quantize_q(0, 2), lambda: scale_mask(2)],
             7: [lambda: interleave_q(1, 2, vcopy)],
-            8: [lambda: quantize_q(1, 2), lambda: interleave_v(0)],
-            9: [lambda: interleave_v(1), lambda: gates(1, 0, H)],
-            10: [quantize_v, lambda: scale_mask(3), lambda: gates(2, 0, H)],
-            11: [lambda: denominators(0), lambda: gates(3, 0, H)],
+            8: [lambda: quantize_q(1, 2), sign_v],
+            9: [interleave_v, lambda: gates(1, 0, H)],
+            10: [quantize_v, lambda: scale_mask(3)],
+            11: [lambda: denominators(0), lambda: gates(2, 0, H)],
             12: [lambda: reciprocals(0), lambda: denominators(1)],
             13: [lambda: reciprocals(1), lambda: finish(0)],
             14: [lambda: finish(1)],
-            15: [lambda: denominators(2)],
-            16: [lambda: reciprocals(2)],
-            17: [lambda: finish(2)],
+            16: [lambda: denominators(2)],
+            17: [lambda: reciprocals(2)],
+            18: [lambda: finish(2)],
         }
 
         scores(0)
-        interleave_q(1, 0, nc.scalar.copy)
+        interleave_q(1, 0, vcopy)
         quantize_q(1, 0)
-        scale_mask(0)
         scores(1)
+        scale_mask(0)
         interleave_q(0, 1, vcopy)
         count = len(units)
-        mixed = 0
-        on_vector = ()
-        for i in range(count + 2):
-            if 0 <= i - 2 < count and i - 2 not in on_vector:
-                square(i - 2)
+        done = {"square": 0, "quantize": 0, "mix": 0}
+        for i in range(count + 3):
+            lag = 2 if i < 4 else 3
+            if done["square"] <= i - lag:
+                square(done["square"])
+                done["square"] = done["square"] + 1
             if 0 <= i - 1 < count:
                 weigh(i - 1)
             if i < count:
                 cap(i)
-            if i - 2 in on_vector:
-                nc.vector.tensor_tensor(out=new_squared(i - 2), in0=scaled[i - 2][:], in1=scaled[i - 2][:], op=ALU.mult)
-            if 0 <= i - 3 < count:
-                quantize_w(i - 3)
+            if done["quantize"] <= i - lag - 1:
+                quantize_w(done["quantize"])
+                done["quantize"] = done["quantize"] + 1
             for step in extra.get(i, []):
                 step()
             if 1 <= i and i + 2 < count:
                 scores(i + 2)
-            while i >= 10 and mixed <= i - 3:
-                mix(mixed)
-                mixed = mixed + 1
+            while i >= 10 and done["mix"] < done["quantize"]:
+                mix(done["mix"])
+                done["mix"] = done["mix"] + 1
+        gates(3, 0, H)
         quantize_w(count - 1)
         mix(count - 1)
         denominators(3)
         reciprocals(3)
-        denominators(4)
         finish(3)
+        denominators(4)
         reciprocals(4)
         finish(4)

@@ -19,21 +19,20 @@ PACK = 4
 ROWS = D // PACK
 QT = 128
 TILES = NQ // QT
-HALF = N // 2
-SLOTS = HALF // PACK
-LATE = True
+RUN = 4
 
 
 def tile_rows_a_relu2_mask_cap_gate_kernel(tc, qT, kT, t, v, mask, og, out):
     nc = tc.nc
     q_rows = qT.rearrange("(g h) (p j) n -> g (h p) j n", h=2, j=PACK)
-    k_rows = kT.rearrange("h (p j) n -> (h p) j n", j=PACK)
-    mask_rows = mask.rearrange("(p j) n -> p j n", j=PACK)
-    og_rows = og.rearrange("h (c m) e -> c m h e", m=QT)
-    out_rows = out.rearrange("h (c m) e -> c m h e", m=QT)
+    og_rows = og.rearrange("h (c m) e -> m (h c) e", m=QT)
+    out_rows = out.rearrange("h (c m) e -> h m c e", m=QT)
 
-    units = [(0, 0), (3, 0), (0, 1), (1, 0), (2, 0), (1, 1), (2, 1), (3, 1)] + [(h, c) for c in range(2, TILES) for h in range(H)]
-    groups = [(0, 0, 4), (1, 0, 4), (2, 0, 4), (3, 0, 3), (3, 3, 4)]
+    units = [(0, 0), (0, 1), (1, 0), (1, 1)] + [(h, c) for c in (2, 3) for h in (0, 1)] + [(h, c) for c in range(TILES) for h in (2, 3)]
+    count = len(units)
+    groups = [range(0, 4), range(4, 8), range(8, 12), range(12, 15), range(15, 16)]
+    blocks = [[0], [1], [2], [3]] + [[u, u + 1] for u in range(4, count, 2)]
+    early = ()
 
     with ExitStack() as ctx:
         keep = ctx.enter_context(tc.tile_pool(name="keep", bufs=1))
@@ -41,7 +40,7 @@ def tile_rows_a_relu2_mask_cap_gate_kernel(tc, qT, kT, t, v, mask, og, out):
         psum = ctx.enter_context(tc.psum_pool(name="psum", bufs=2))
         ctx.enter_context(tc.manual_schedule())
 
-        def load(name, src, queue=nc.sync):
+        def load(name, src, queue):
             dst = keep.tile(list(src.shape), F32, name=name)
             queue.dma_start(out=dst[:], in_=src)
             return dst
@@ -49,39 +48,31 @@ def tile_rows_a_relu2_mask_cap_gate_kernel(tc, qT, kT, t, v, mask, og, out):
         def planes(name, width):
             return keep.tile([P, width + width // 4], I32, name=name, align_bytes=64)
 
-        def codes(pl, width, rows, c0, n):
+        def codes(pl, rows, c0, n):
             return pl[rows, c0 : c0 + n].bitcast(FP8X4)
 
-        def scales(pl, width, rows, c0, n):
+        def scales(pl, rows, c0, n):
+            width = pl.shape[1] * 4 // 5
             return pl[rows, width + c0 // 4 : width + (c0 + n) // 4].bitcast(U8)
 
         every = slice(0, P)
 
-        def quantize(pl, width, c0, src):
+        def quantize(pl, src):
             n = src.shape[1] // PACK
-            nc.vector.quantize_mx(out=codes(pl, width, every, c0, n), scales=scales(pl, width, every, c0, n), in_=src)
-
-        q_raw, m_raw, og_raw = {}, {}, {}
-
-        def load_q(g, c, n):
-            q_raw[g, c] = load("q_raw%d%d" % (g, c), q_rows[g][:, :, c * QT : (c + n) * QT])
-
-        def load_mask(c, n):
-            raw = load("m_raw%d" % c, mask_rows[:, :, c * QT : (c + n) * QT])
-            for i in range(n):
-                m_raw[c + i] = raw[:, :, i * QT : (i + 1) * QT]
-
-        def load_og(c, lo, hi, queue=nc.sync):
-            og_raw[c, lo] = load("og_raw%d%d" % (c, lo), og_rows[c][:, lo:hi, :], queue)
+            nc.vector.quantize_mx(out=codes(pl, every, 0, n), scales=scales(pl, every, 0, n), in_=src)
 
         t_sb = load("t_sb", t.rearrange("(p j) o -> p (j o)", j=PACK), nc.scalar)
-        load_og(0, 0, 1, nc.scalar)
-        k_raw = [load("k_raw0", k_rows[:, :, 0:HALF])]
-        load_q(0, 0, 1)
-        k_raw.append(load("k_raw1", k_rows[:, :, HALF:N]))
-        load_q(1, 0, 1)
-        load_mask(0, 1)
-        load_q(0, 1, 1)
+        og_first = load("og_first", og_rows[:, 0:1, :], nc.scalar)
+        k_raw = load("k_raw", kT.rearrange("h (p j) n -> (h p) j n", j=PACK), nc.sync)
+        q_all = [load("q_all0", q_rows[0], nc.sync)]
+        m_raw = load("m_raw", mask.rearrange("(p j) n -> p j n", j=PACK), nc.sync)
+        q_all.append(load("q_all1", q_rows[1], nc.sync))
+        v_raw = load("v_raw", v.rearrange("h (p j) e -> p h (j e)", j=PACK), nc.sync)
+        og_a = load("og_a", og_rows[:, 1 : 2 * TILES, :], nc.sync)
+
+        def q_raw(g, c, n):
+            return q_all[g][:, :, c * QT : (c + n) * QT]
+
 
         k_pl = planes("k_pl", N)
         k_swapped = planes("k_swapped", N)
@@ -93,227 +84,236 @@ def tile_rows_a_relu2_mask_cap_gate_kernel(tc, qT, kT, t, v, mask, og, out):
         inverse = keep.tile([P, PACK], F32)
         quotient = keep.tile([P, PACK], F32)
         root = keep.tile([P, PACK], F32)
-        gate = keep.tile([P, TILES, H, E], F32)
-
-        def gates(c, lo, hi):
-            nc.scalar.activation(out=gate[:, c, lo:hi, :], in_=og_raw[c, lo][:], func=ACT.Sigmoid)
+        gate = keep.tile([P, H * TILES, E], F32)
 
         nc.vector.scalar_tensor_tensor(out=t_abs[:], in0=t_sb[:], scalar=-1.0, in1=t_sb[:], op0=ALU.mult, op1=ALU.max)
         nc.scalar.activation(out=guess[:], in_=t_abs[:], func=ACT.Sqrt, scale=CAP * CAP)
         nc.scalar.activation(out=t_sign[:], in_=t_sb[:], func=ACT.Sign)
-        gates(0, 0, 1)
+        nc.scalar.activation(out=gate[:, 0:1, :], in_=og_first[:], func=ACT.Sigmoid)
         nc.vector.reciprocal(out=inverse[:], in_=guess[:])
         nc.vector.scalar_tensor_tensor(out=quotient[:], in0=inverse[:], scalar=0.5 * CAP * CAP, in1=t_abs[:], op0=ALU.mult, op1=ALU.mult)
         nc.vector.scalar_tensor_tensor(out=root[:], in0=guess[:], scalar=0.5, in1=quotient[:], op0=ALU.mult, op1=ALU.add)
 
-        def interleave_k(a, lo, hi, copy):
+        k_bf = keep.tile([P, PACK, P, PACK], BF16, align_bytes=64)
+
+        def interleave_k(lo, hi, copy):
             copy(
-                out=k_bf[a][:, :, lo:hi, :].rearrange("p r s j -> p s j r"),
-                in_=k_raw[a][:, :, lo * PACK : hi * PACK].rearrange("p j (s r) -> p s j r", r=PACK),
+                out=k_bf[:, :, lo:hi, :].rearrange("p r s j -> p s j r"),
+                in_=k_raw[:, :, lo * PACK : hi * PACK].rearrange("p j (s r) -> p s j r", r=PACK),
             )
 
-        def quantize_k(a):
-            for r in range(PACK):
-                quantize(k_pl, N, r * P + a * SLOTS, k_bf[a][:, r, :, :].rearrange("p s j -> p (s j)"))
+        q_bf, q_pl = {}, {}
 
-        q_bf = {}
-        q_pl = {}
-
-        def interleave_q(g, c, copy):
-            raw = q_raw[g, c]
-            qb = keep.tile([P, raw.shape[2] * PACK], BF16, name="q_bf%d%d" % (g, c), align_bytes=64)
-            copy(out=qb[:].rearrange("p (c i j) -> p c j i", i=4, j=PACK), in_=raw[:].rearrange("p j (c i) -> p c j i", i=4))
+        def interleave_q(g, c, n, copy):
+            qb = keep.tile([P, n * QT * PACK], BF16, name="q_bf%d%d" % (g, c), align_bytes=64)
+            copy(
+                out=qb[:].rearrange("p (b i j) -> p b j i", i=RUN, j=PACK),
+                in_=q_raw(g, c, n).rearrange("p j (b i) -> p b j i", i=RUN),
+            )
             q_bf[g, c] = qb
 
         def quantize_q(g, c):
-            width = q_raw[g, c].shape[2]
+            width = q_bf[g, c].shape[1] // PACK
             pl = planes("q_pl%d%d" % (g, c), width)
-            quantize(pl, width, 0, q_bf[g, c][:])
+            quantize(pl, q_bf[g, c][:])
             for i in range(width // QT):
-                q_pl[g, c + i] = (pl, width, i * QT)
+                q_pl[g, c + i] = (pl, i * QT)
 
-        weight = {}
+        weight = keep.tile([P, PACK, NQ], F32)
+        woven = {}
 
-        def scale_mask(c):
-            ms = keep.tile([P, QT * PACK], F32, name="weight%d" % c)
-            if LATE:
-                for j in range(PACK):
-                    nc.vector.tensor_scalar(out=ms[:, j * QT : (j + 1) * QT], in0=m_raw[c][:, j, :], scalar1=root[:, j : j + 1], scalar2=None, op0=ALU.mult)
-            else:
-                nc.vector.tensor_tensor(
-                    out=ms[:].rearrange("p (c i j) -> p c j i", i=4, j=PACK),
-                    in0=m_raw[c].rearrange("p j (c i) -> p c j i", i=4),
-                    in1=root[:].unsqueeze(1).unsqueeze(3).to_broadcast([P, QT // 4, PACK, 4]),
-                    op=ALU.mult,
-                )
-            weight[c] = ms
+        def scale_mask(c, n):
+            cols = slice(c * QT, (c + n) * QT)
+            for j in range(PACK):
+                nc.vector.tensor_scalar(out=weight[:, j, cols], in0=m_raw[:, j, cols], scalar1=root[:, j : j + 1], scalar2=None, op0=ALU.mult)
 
-        k_bf = [keep.tile([P, PACK, SLOTS, PACK], BF16, name="k_bf%d" % a, align_bytes=64) for a in range(2)]
-        interleave_k(0, 0, SLOTS, nc.vector.tensor_copy)
-        quantize_k(0)
-        interleave_q(0, 0, nc.scalar.copy)
-        interleave_k(1, 0, 44, nc.vector.tensor_copy)
-        interleave_k(1, 44, SLOTS, nc.scalar.copy)
-        quantize_q(0, 0)
-        quantize_k(1)
+        def weave(c):
+            woven[c] = keep.tile([P, QT * PACK], F32, name="woven%d" % c)
+            nc.vector.tensor_copy(
+                out=woven[c][:].rearrange("p (q j) -> p q j", j=PACK), in_=weight[:, :, c * QT : (c + 1) * QT].rearrange("p j q -> p q j")
+            )
+
+        vcopy = nc.vector.tensor_copy
+        interleave_k(0, 88, vcopy)
+        interleave_k(88, P, nc.scalar.copy)
+        quantize(k_pl, k_bf[:].rearrange("p r s j -> p (r s j)"))
         nc.scalar.dma_start(out=k_swapped[ROWS:P, :], in_=k_pl[0:ROWS, :])
-        nc.scalar.dma_start(out=k_swapped[0:ROWS, :], in_=k_pl[ROWS:P, :])
-
-        load_mask(1, 1)
-        load_q(1, 1, 1)
-        load_q(0, 2, 2)
-        load_og(0, 1, H)
-        load_mask(2, 2)
-        load_q(1, 2, 2)
-        v_raw = load("v_raw", v.rearrange("h (p j) e -> p h (j e)", j=PACK))
-        for c in range(1, TILES):
-            load_og(c, 0, H)
-
-        v_bf = keep.tile([P, KV, E * PACK], BF16, align_bytes=64)
-        v_pl = planes("v_pl", KV * E)
+        nc.sync.dma_start(out=k_swapped[0:ROWS, :], in_=k_pl[ROWS:P, :])
+        og_b = load("og_b", og_rows[:, 2 * TILES :, :], nc.sync)
+        interleave_q(0, 0, 1, vcopy)
+        interleave_q(0, 1, 1, nc.scalar.copy)
+        quantize_q(0, 0)
 
         v_signed = keep.tile([P, KV, PACK, E], F32)
+        v_bf = keep.tile([P, KV * E * PACK], BF16, align_bytes=64)
+        v_pl = planes("v_pl", KV * E)
 
         def sign_v():
             for j in range(PACK):
-                nc.vector.tensor_scalar(out=v_signed[:, :, j, :], in0=v_raw[:, :, j * E : (j + 1) * E], scalar1=t_sign[:, j : j + 1], scalar2=None, op0=ALU.mult)
+                nc.vector.tensor_scalar(
+                    out=v_signed[:, :, j, :], in0=v_raw[:, :, j * E : (j + 1) * E], scalar1=t_sign[:, j : j + 1], scalar2=None, op0=ALU.mult
+                )
 
         def interleave_v():
             nc.vector.tensor_copy(
-                out=v_bf[:].rearrange("p g (c i j) -> p g c j i", i=4, j=PACK), in_=v_signed[:].rearrange("p g j (c i) -> p g c j i", i=4)
+                out=v_bf[:].rearrange("p (g b i j) -> p g b j i", g=KV, i=RUN, j=PACK),
+                in_=v_signed[:].rearrange("p g j (b i) -> p g b j i", i=RUN),
             )
-
-        def quantize_v():
-            quantize(v_pl, KV * E, 0, v_bf[:].rearrange("p g n -> p (g n)"))
 
         banks, capped, scaled, squared, w_pl, sums = {}, {}, {}, {}, {}, {}
 
-        def scores(u):
-            h, c = units[u]
-            rows = slice(ROWS * (h % 2), ROWS * (h % 2 + 1))
-            keys = k_pl if h // 2 == h % 2 else k_swapped
-            pl, width, c0 = q_pl[h // 2, c]
-            bank = psum.tile([P, PACK, QT], F32, name="scores%d" % (h % 2))
+        def scores(block):
+            for u in block:
+                banks[u] = psum.tile([P, PACK, QT], F32, name="scores%d" % (units[u][0] % 2))
             for r in range(PACK):
-                nc.tensor.matmul_mx(
-                    out=bank[:, r, :],
-                    lhsT=codes(keys, N, rows, r * P, P),
-                    lhsT_scale=scales(keys, N, rows, r * P, P),
-                    rhs=codes(pl, width, rows, c0, QT),
-                    rhs_scale=scales(pl, width, rows, c0, QT),
-                    start=True,
-                    stop=True,
-                )
-            banks[u] = bank
+                for u in block:
+                    h, c = units[u]
+                    rows = slice(ROWS * (h % 2), ROWS * (h % 2 + 1))
+                    keys = k_pl if h // 2 == h % 2 else k_swapped
+                    pl, c0 = q_pl[h // 2, c]
+                    nc.tensor.matmul_mx(
+                        out=banks[u][:, r, :],
+                        lhsT=codes(keys, rows, r * P, P),
+                        lhsT_scale=scales(keys, rows, r * P, P),
+                        rhs=codes(pl, rows, c0, QT),
+                        rhs_scale=scales(pl, rows, c0, QT),
+                        start=True,
+                        stop=True,
+                    )
 
         def cap(u):
-            th = work.tile([P, QT * PACK], F32, name="capped")
-            if LATE:
-                nc.scalar.activation(out=th[:], in_=banks[u][:].rearrange("p r q -> p (r q)"), func=ACT.Tanh, scale=1.0 / CAP)
-            else:
+            capped[u] = work.tile([P, QT * PACK], F32, name="capped")
+            if u in early:
                 nc.scalar.activation(
-                    out=th[:].rearrange("p (q r) -> p q r", r=PACK), in_=banks[u][:].rearrange("p r q -> p q r"), func=ACT.Tanh, scale=1.0 / CAP
+                    out=capped[u][:].rearrange("p (q r) -> p q r", r=PACK), in_=banks[u][:].rearrange("p r q -> p q r"), func=ACT.Tanh, scale=1.0 / CAP
                 )
-            capped[u] = th
+            else:
+                nc.scalar.activation(out=capped[u][:], in_=banks[u][:].rearrange("p r q -> p (r q)"), func=ACT.Tanh, scale=1.0 / CAP)
 
         def weigh(u):
-            x = work.tile([P, QT * PACK], F32, name="scaled")
-            nc.vector.scalar_tensor_tensor(out=x[:], in0=capped[u][:], scalar=0.0, in1=weight[units[u][1]][:], op0=ALU.max, op1=ALU.mult)
-            scaled[u] = x
+            c = units[u][1]
+            scaled[u] = work.tile([P, QT * PACK], F32, name="scaled")
+            if u in early:
+                nc.vector.scalar_tensor_tensor(out=scaled[u][:], in0=capped[u][:], scalar=0.0, in1=woven[c][:], op0=ALU.max, op1=ALU.mult)
+            else:
+                nc.vector.scalar_tensor_tensor(
+                    out=scaled[u][:].rearrange("p (r q) -> p r q", r=PACK),
+                    in0=capped[u][:].rearrange("p (r q) -> p r q", r=PACK),
+                    scalar=0.0,
+                    in1=weight[:, :, c * QT : (c + 1) * QT],
+                    op0=ALU.max,
+                    op1=ALU.mult,
+                )
 
         def square(u):
-            wb = work.tile([P, QT * PACK], BF16, name="squared", align_bytes=64)
-            if LATE:
+            squared[u] = work.tile([P, QT * PACK], BF16, name="squared", align_bytes=64)
+            if u in on_vector:
+                nc.vector.tensor_tensor(out=squared[u][:], in0=scaled[u][:], in1=scaled[u][:], op=ALU.mult)
+            elif u in early:
+                nc.scalar.activation(out=squared[u][:], in_=scaled[u][:], func=ACT.Square)
+            else:
                 nc.scalar.activation(
-                    out=wb[:].rearrange("p (c i r) -> p c r i", i=4, r=PACK),
-                    in_=scaled[u][:].rearrange("p (r c i) -> p c r i", i=4, r=PACK),
+                    out=squared[u][:].rearrange("p (b i r) -> p b r i", i=RUN, r=PACK),
+                    in_=scaled[u][:].rearrange("p (r b i) -> p b r i", i=RUN, r=PACK),
                     func=ACT.Square,
                 )
-            else:
-                nc.scalar.activation(out=wb[:], in_=scaled[u][:], func=ACT.Square)
-            squared[u] = wb
-
-        def new_squared(u):
-            squared[u] = work.tile([P, QT * PACK], BF16, name="squared", align_bytes=64)
-            return squared[u][:]
 
         def quantize_w(u):
             w_pl[u] = planes("w_pl%d" % u, QT)
-            quantize(w_pl[u], QT, 0, squared[u][:])
+            quantize(w_pl[u], squared[u][:])
+
+        def slot(u):
+            return 2 * (units[u][0] % 2) + units[u][1] % 2
 
         def mix(u):
-            h, c = units[u]
-            g = [i for i, (cc, lo, hi) in enumerate(groups) if cc == c and lo <= h < hi][0]
+            g = [i for i, members in enumerate(groups) if u in members][0]
             if g not in sums:
-                sums[g] = psum.tile([P, H, E], F32, name="sums", bufs=4)
+                sums[g] = psum.tile([P, 4, E], F32, name="sums", bufs=4)
+            e0 = (units[u][0] // 2) * E
             nc.tensor.matmul_mx(
-                out=sums[g][:, h, :],
-                lhsT=codes(w_pl[u], QT, every, 0, QT),
-                lhsT_scale=scales(w_pl[u], QT, every, 0, QT),
-                rhs=codes(v_pl, KV * E, every, (h // 2) * E, E),
-                rhs_scale=scales(v_pl, KV * E, every, (h // 2) * E, E),
+                out=sums[g][:, slot(u), :],
+                lhsT=codes(w_pl[u], every, 0, QT),
+                lhsT_scale=scales(w_pl[u], every, 0, QT),
+                rhs=codes(v_pl, every, e0, E),
+                rhs_scale=scales(v_pl, every, e0, E),
                 start=True,
                 stop=True,
             )
 
         dens, recs = {}, {}
 
+        def span(g):
+            used = [slot(u) for u in groups[g]]
+            return slice(min(used), max(used) + 1)
+
         def denominators(g):
-            c, lo, hi = groups[g]
-            dens[g] = keep.tile([P, H], F32, name="den%d" % g)
-            nc.vector.tensor_scalar(out=dens[g][:, lo:hi], in0=sums[g][:, lo:hi, E - 1], scalar1=1.0, scalar2=None, op0=ALU.add)
+            dens[g] = keep.tile([P, 4], F32, name="den%d" % g)
+            nc.vector.tensor_scalar(out=dens[g][:, span(g)], in0=sums[g][:, span(g), E - 1], scalar1=1.0, scalar2=None, op0=ALU.add)
 
         def reciprocals(g):
-            c, lo, hi = groups[g]
-            recs[g] = keep.tile([P, H], F32, name="rec%d" % g)
-            nc.vector.reciprocal(out=recs[g][:, lo:hi], in_=dens[g][:, lo:hi])
+            recs[g] = keep.tile([P, 4], F32, name="rec%d" % g)
+            nc.vector.reciprocal(out=recs[g][:, span(g)], in_=dens[g][:, span(g)])
 
         def finish(g):
-            c, lo, hi = groups[g]
-            res = keep.tile([P, hi - lo, E], F32, name="res%d" % g)
-            for h in range(lo, hi):
-                nc.vector.scalar_tensor_tensor(
-                    out=res[:, h - lo, :],
-                    in0=sums[g][:, h, :],
-                    scalar=recs[g][:, h : h + 1],
-                    in1=gate[:, c, h, :],
-                    op0=ALU.mult,
-                    op1=ALU.mult,
-                )
-            nc.sync.dma_start(out=out_rows[c][:, lo:hi, :], in_=res[:])
+            for h in sorted(set(units[u][0] for u in groups[g])):
+                members = [u for u in groups[g] if units[u][0] == h]
+                c0 = units[members[0]][1]
+                res = keep.tile([P, len(members), E], F32, name="res%d%d" % (g, h))
+                for i, u in enumerate(members):
+                    nc.vector.scalar_tensor_tensor(
+                        out=res[:, i, :],
+                        in0=sums[g][:, slot(u), :],
+                        scalar=recs[g][:, slot(u) : slot(u) + 1],
+                        in1=gate[:, h * TILES + c0 + i, :],
+                        op0=ALU.mult,
+                        op1=ALU.mult,
+                    )
+                nc.sync.dma_start(out=out_rows[h][:, c0 : c0 + len(members), :], in_=res[:])
 
-        vcopy = nc.vector.tensor_copy
+        def gates_a(lo, hi):
+            nc.scalar.activation(out=gate[:, lo:hi, :], in_=og_a[:, lo - 1 : hi - 1, :], func=ACT.Sigmoid)
+
+        def gates_b(c0):
+            nc.scalar.activation(
+                out=gate[:, 2 * TILES :, :].rearrange("p (h c) e -> p h c e", h=2)[:, :, c0 : c0 + 2, :],
+                in_=og_b[:].rearrange("p (h c) e -> p h c e", h=2)[:, :, c0 : c0 + 2, :],
+                func=ACT.Sigmoid,
+            )
+
+        on_vector = ()
         extra = {
-            1: [lambda: quantize_q(0, 1), lambda: scores(2)],
-            2: [lambda: scale_mask(1)],
-            3: [lambda: interleave_q(1, 1, vcopy)],
-            4: [lambda: quantize_q(1, 1)],
-            5: [lambda: interleave_q(0, 2, vcopy), lambda: gates(0, 1, H)],
-            6: [lambda: quantize_q(0, 2), lambda: scale_mask(2)],
-            7: [lambda: interleave_q(1, 2, vcopy)],
-            8: [lambda: quantize_q(1, 2), sign_v],
-            9: [interleave_v, lambda: gates(1, 0, H)],
-            10: [quantize_v, lambda: scale_mask(3)],
-            11: [lambda: denominators(0), lambda: gates(2, 0, H)],
-            12: [lambda: reciprocals(0), lambda: denominators(1)],
-            13: [lambda: reciprocals(1), lambda: finish(0)],
+            1: [lambda: scale_mask(1, 1)],
+            2: [lambda: scale_mask(2, 2)],
+            4: [lambda: interleave_q(1, 0, 2, vcopy)],
+            5: [lambda: quantize_q(1, 0), sign_v],
+            6: [interleave_v, lambda: gates_a(1, 4)],
+            7: [lambda: quantize(v_pl, v_bf[:]), lambda: interleave_q(1, 2, 2, vcopy), lambda: gates_a(4, 8)],
+            8: [lambda: quantize_q(1, 2)],
+            9: [lambda: denominators(0), lambda: gates_b(0)],
+            10: [lambda: reciprocals(0)],
+            11: [lambda: finish(0)],
+            12: [lambda: denominators(1)],
+            13: [lambda: reciprocals(1)],
             14: [lambda: finish(1)],
             16: [lambda: denominators(2)],
             17: [lambda: reciprocals(2)],
             18: [lambda: finish(2)],
         }
 
-        scores(0)
-        interleave_q(1, 0, vcopy)
-        quantize_q(1, 0)
-        scores(1)
-        scale_mask(0)
-        interleave_q(0, 1, vcopy)
-        count = len(units)
-        done = {"square": 0, "quantize": 0, "mix": 0}
+        def previous(u):
+            same = [x for x in range(u) if units[x][0] % 2 == units[u][0] % 2]
+            return same[-2] if len(same) >= 2 else -1
+
+        scores(blocks[0])
+        interleave_q(0, 2, 2, vcopy)
+        quantize_q(0, 1)
+        scores(blocks[1])
+        quantize_q(0, 2)
+        scale_mask(0, 1)
+        done = {"square": 0, "quantize": 0, "mix": 0, "block": 2}
         for i in range(count + 3):
-            lag = 2 if i < 4 else 3
-            if done["square"] <= i - lag:
+            lag = 2 if i < 0 else 3
+            if done["square"] <= i - lag and done["square"] not in on_vector:
                 square(done["square"])
                 done["square"] = done["square"] + 1
             if 0 <= i - 1 < count:
@@ -323,14 +323,18 @@ def tile_rows_a_relu2_mask_cap_gate_kernel(tc, qT, kT, t, v, mask, og, out):
             if done["quantize"] <= i - lag - 1:
                 quantize_w(done["quantize"])
                 done["quantize"] = done["quantize"] + 1
+            if done["square"] <= i - lag:
+                square(done["square"])
+                done["square"] = done["square"] + 1
             for step in extra.get(i, []):
                 step()
-            if 1 <= i and i + 2 < count:
-                scores(i + 2)
-            while i >= 10 and done["mix"] < done["quantize"]:
+            while done["block"] < len(blocks) and max(previous(u) for u in blocks[done["block"]]) <= i:
+                scores(blocks[done["block"]])
+                done["block"] = done["block"] + 1
+            while i >= 8 and done["mix"] < done["quantize"]:
                 mix(done["mix"])
                 done["mix"] = done["mix"] + 1
-        gates(3, 0, H)
+        gates_b(2)
         quantize_w(count - 1)
         mix(count - 1)
         denominators(3)

@@ -20,6 +20,13 @@ ROWS = D // PACK
 QT = 128
 TILES = NQ // QT
 RUN = 4
+K_ON_VECTOR = 88
+SCORE_BANKS = 3
+SUM_BANKS = 2
+AHEAD = 2
+SQUARE_LAG = 3
+WORK_BUFS = SQUARE_LAG + 2
+FIRST_SIDE_STEP = 4
 
 
 def tile_rows_a_relu2_mask_cap_gate_kernel(tc, qT, kT, t, v, mask, og, out):
@@ -28,16 +35,16 @@ def tile_rows_a_relu2_mask_cap_gate_kernel(tc, qT, kT, t, v, mask, og, out):
     og_rows = og.rearrange("h (c m) e -> m (h c) e", m=QT)
     out_rows = out.rearrange("h (c m) e -> h m c e", m=QT)
 
-    units = [(0, 0), (0, 1), (1, 0), (1, 1)] + [(h, c) for c in (2, 3) for h in (0, 1)] + [(h, c) for c in range(TILES) for h in (2, 3)]
+    units = [(h, c) for h in (0, 1) for c in range(TILES)] + [(h, c) for c in range(TILES) for h in (2, 3)]
     count = len(units)
-    groups = [range(0, 4), range(4, 8), range(8, 12), range(12, 15), range(15, 16)]
-    blocks = [[0], [1], [2], [3]] + [[u, u + 1] for u in range(4, count, 2)]
-    early = ()
+    half = count // 2
+    blocks = [[u] for u in range(half)] + [[u, u + 1] for u in range(half, count, 2)]
+    groups = [range(0, 4), range(4, 8), range(8, 12), range(12, 14), range(14, 16)]
 
     with ExitStack() as ctx:
         keep = ctx.enter_context(tc.tile_pool(name="keep", bufs=1))
-        work = ctx.enter_context(tc.tile_pool(name="work", bufs=5))
-        psum = ctx.enter_context(tc.psum_pool(name="psum", bufs=2))
+        work = ctx.enter_context(tc.tile_pool(name="work", bufs=WORK_BUFS))
+        psum = ctx.enter_context(tc.psum_pool(name="psum", bufs=1))
         ctx.enter_context(tc.manual_schedule())
 
         def load(name, src, queue):
@@ -45,38 +52,31 @@ def tile_rows_a_relu2_mask_cap_gate_kernel(tc, qT, kT, t, v, mask, og, out):
             queue.dma_start(out=dst[:], in_=src)
             return dst
 
-        def planes(name, width):
+        def new_operand(name, width):
             return keep.tile([P, width + width // 4], I32, name=name, align_bytes=64)
 
-        def codes(pl, rows, c0, n):
-            return pl[rows, c0 : c0 + n].bitcast(FP8X4)
+        def codes(operand, rows, c0, n):
+            return operand[rows, c0 : c0 + n].bitcast(FP8X4)
 
-        def scales(pl, rows, c0, n):
-            width = pl.shape[1] * 4 // 5
-            return pl[rows, width + c0 // 4 : width + (c0 + n) // 4].bitcast(U8)
+        def scales(operand, rows, c0, n):
+            width = operand.shape[1] * 4 // 5
+            return operand[rows, width + c0 // 4 : width + (c0 + n) // 4].bitcast(U8)
 
         every = slice(0, P)
 
-        def quantize(pl, src):
+        def quantize(operand, src):
             n = src.shape[1] // PACK
-            nc.vector.quantize_mx(out=codes(pl, every, 0, n), scales=scales(pl, every, 0, n), in_=src)
+            nc.vector.quantize_mx(out=codes(operand, every, 0, n), scales=scales(operand, every, 0, n), in_=src)
 
         t_sb = load("t_sb", t.rearrange("(p j) o -> p (j o)", j=PACK), nc.scalar)
         og_first = load("og_first", og_rows[:, 0:1, :], nc.scalar)
         k_raw = load("k_raw", kT.rearrange("h (p j) n -> (h p) j n", j=PACK), nc.sync)
-        q_all = [load("q_all0", q_rows[0], nc.sync)]
-        m_raw = load("m_raw", mask.rearrange("(p j) n -> p j n", j=PACK), nc.sync)
-        q_all.append(load("q_all1", q_rows[1], nc.sync))
-        v_raw = load("v_raw", v.rearrange("h (p j) e -> p h (j e)", j=PACK), nc.sync)
-        og_a = load("og_a", og_rows[:, 1 : 2 * TILES, :], nc.sync)
+        q_raw = [load("q_raw0", q_rows[0], nc.sync)]
+        mask_raw = load("mask_raw", mask.rearrange("(p j) n -> p j n", j=PACK), nc.sync)
 
-        def q_raw(g, c, n):
-            return q_all[g][:, :, c * QT : (c + n) * QT]
-
-
-        k_pl = planes("k_pl", N)
-        k_swapped = planes("k_swapped", N)
-        nc.vector.memset(k_pl[:, N : N + N // 4], 0)
+        k_mx = new_operand("k_mx", N)
+        k_swapped = new_operand("k_swapped", N)
+        nc.vector.memset(k_mx[:, N : N + N // 4], 0)
 
         t_abs = keep.tile([P, PACK], F32)
         guess = keep.tile([P, PACK], F32)
@@ -85,174 +85,142 @@ def tile_rows_a_relu2_mask_cap_gate_kernel(tc, qT, kT, t, v, mask, og, out):
         quotient = keep.tile([P, PACK], F32)
         root = keep.tile([P, PACK], F32)
         gate = keep.tile([P, H * TILES, E], F32)
-
         nc.vector.scalar_tensor_tensor(out=t_abs[:], in0=t_sb[:], scalar=-1.0, in1=t_sb[:], op0=ALU.mult, op1=ALU.max)
         nc.scalar.activation(out=guess[:], in_=t_abs[:], func=ACT.Sqrt, scale=CAP * CAP)
         nc.scalar.activation(out=t_sign[:], in_=t_sb[:], func=ACT.Sign)
         nc.scalar.activation(out=gate[:, 0:1, :], in_=og_first[:], func=ACT.Sigmoid)
         nc.vector.reciprocal(out=inverse[:], in_=guess[:])
-        nc.vector.scalar_tensor_tensor(out=quotient[:], in0=inverse[:], scalar=0.5 * CAP * CAP, in1=t_abs[:], op0=ALU.mult, op1=ALU.mult)
+        nc.vector.scalar_tensor_tensor(
+            out=quotient[:], in0=inverse[:], scalar=0.5 * CAP * CAP, in1=t_abs[:], op0=ALU.mult, op1=ALU.mult
+        )
         nc.vector.scalar_tensor_tensor(out=root[:], in0=guess[:], scalar=0.5, in1=quotient[:], op0=ALU.mult, op1=ALU.add)
 
         k_bf = keep.tile([P, PACK, P, PACK], BF16, align_bytes=64)
-
-        def interleave_k(lo, hi, copy):
+        for lo, hi, copy in ((0, K_ON_VECTOR, nc.vector.tensor_copy), (K_ON_VECTOR, P, nc.scalar.copy)):
             copy(
                 out=k_bf[:, :, lo:hi, :].rearrange("p r s j -> p s j r"),
                 in_=k_raw[:, :, lo * PACK : hi * PACK].rearrange("p j (s r) -> p s j r", r=PACK),
             )
+        quantize(k_mx, k_bf[:].rearrange("p r s j -> p (r s j)"))
 
-        q_bf, q_pl = {}, {}
+        nc.sync.dma_start(out=k_swapped[ROWS:P, :], in_=k_mx[0:ROWS, :])
+        q_raw.append(load("q_raw1", q_rows[1], nc.sync))
+        v_raw = load("v_raw", v.rearrange("h (p j) e -> p h (j e)", j=PACK), nc.sync)
+        nc.sync.dma_start(out=k_swapped[0:ROWS, :], in_=k_mx[ROWS:P, :])
+        og_low = load("og_low", og_rows[:, 1 : 2 * TILES, :], nc.sync)
+        og_high = load("og_high", og_rows[:, 2 * TILES :, :], nc.sync)
+
+        q_bf, q_mx = {}, {}
 
         def interleave_q(g, c, n, copy):
-            qb = keep.tile([P, n * QT * PACK], BF16, name="q_bf%d%d" % (g, c), align_bytes=64)
+            q_bf[g, c] = keep.tile([P, n * QT * PACK], BF16, name="q_bf%d%d" % (g, c), align_bytes=64)
             copy(
-                out=qb[:].rearrange("p (b i j) -> p b j i", i=RUN, j=PACK),
-                in_=q_raw(g, c, n).rearrange("p j (b i) -> p b j i", i=RUN),
+                out=q_bf[g, c][:].rearrange("p (b i j) -> p b j i", i=RUN, j=PACK),
+                in_=q_raw[g][:, :, c * QT : (c + n) * QT].rearrange("p j (b i) -> p b j i", i=RUN),
             )
-            q_bf[g, c] = qb
 
         def quantize_q(g, c):
             width = q_bf[g, c].shape[1] // PACK
-            pl = planes("q_pl%d%d" % (g, c), width)
-            quantize(pl, q_bf[g, c][:])
+            operand = new_operand("q_mx%d%d" % (g, c), width)
+            quantize(operand, q_bf[g, c][:])
             for i in range(width // QT):
-                q_pl[g, c + i] = (pl, i * QT)
+                q_mx[g, c + i] = (operand, i * QT)
 
         weight = keep.tile([P, PACK, NQ], F32)
-        woven = {}
 
         def scale_mask(c, n):
             cols = slice(c * QT, (c + n) * QT)
-            for j in range(PACK):
-                nc.vector.tensor_scalar(out=weight[:, j, cols], in0=m_raw[:, j, cols], scalar1=root[:, j : j + 1], scalar2=None, op0=ALU.mult)
-
-        def weave(c):
-            woven[c] = keep.tile([P, QT * PACK], F32, name="woven%d" % c)
-            nc.vector.tensor_copy(
-                out=woven[c][:].rearrange("p (q j) -> p q j", j=PACK), in_=weight[:, :, c * QT : (c + 1) * QT].rearrange("p j q -> p q j")
-            )
-
-        vcopy = nc.vector.tensor_copy
-        interleave_k(0, 88, vcopy)
-        interleave_k(88, P, nc.scalar.copy)
-        quantize(k_pl, k_bf[:].rearrange("p r s j -> p (r s j)"))
-        nc.scalar.dma_start(out=k_swapped[ROWS:P, :], in_=k_pl[0:ROWS, :])
-        nc.sync.dma_start(out=k_swapped[0:ROWS, :], in_=k_pl[ROWS:P, :])
-        og_b = load("og_b", og_rows[:, 2 * TILES :, :], nc.sync)
-        interleave_q(0, 0, 1, vcopy)
-        interleave_q(0, 1, 1, nc.scalar.copy)
-        quantize_q(0, 0)
+            for r in range(PACK):
+                nc.vector.tensor_scalar(
+                    out=weight[:, r, cols], in0=mask_raw[:, r, cols], scalar1=root[:, r : r + 1], scalar2=None, op0=ALU.mult
+                )
 
         v_signed = keep.tile([P, KV, PACK, E], F32)
         v_bf = keep.tile([P, KV * E * PACK], BF16, align_bytes=64)
-        v_pl = planes("v_pl", KV * E)
+        v_mx = new_operand("v_mx", KV * E)
 
         def sign_v():
-            for j in range(PACK):
+            for r in range(PACK):
                 nc.vector.tensor_scalar(
-                    out=v_signed[:, :, j, :], in0=v_raw[:, :, j * E : (j + 1) * E], scalar1=t_sign[:, j : j + 1], scalar2=None, op0=ALU.mult
+                    out=v_signed[:, :, r, :],
+                    in0=v_raw[:, :, r * E : (r + 1) * E],
+                    scalar1=t_sign[:, r : r + 1],
+                    scalar2=None,
+                    op0=ALU.mult,
                 )
 
         def interleave_v():
             nc.vector.tensor_copy(
-                out=v_bf[:].rearrange("p (g b i j) -> p g b j i", g=KV, i=RUN, j=PACK),
-                in_=v_signed[:].rearrange("p g j (b i) -> p g b j i", i=RUN),
+                out=v_bf[:].rearrange("p (g b i r) -> p g b r i", g=KV, i=RUN, r=PACK),
+                in_=v_signed[:].rearrange("p g r (b i) -> p g b r i", i=RUN),
             )
 
-        banks, capped, scaled, squared, w_pl, sums = {}, {}, {}, {}, {}, {}
+        banks, capped, scaled, squared, w_mx, sums, dens, recs = {}, {}, {}, {}, {}, {}, {}, {}
 
         def scores(block):
             for u in block:
-                banks[u] = psum.tile([P, PACK, QT], F32, name="scores%d" % (units[u][0] % 2))
+                banks[u] = psum.tile([P, PACK, QT], F32, name="scores%d" % (units[u][0] % 2), bufs=SCORE_BANKS)
             for r in range(PACK):
                 for u in block:
                     h, c = units[u]
                     rows = slice(ROWS * (h % 2), ROWS * (h % 2 + 1))
-                    keys = k_pl if h // 2 == h % 2 else k_swapped
-                    pl, c0 = q_pl[h // 2, c]
+                    keys = k_mx if h // 2 == h % 2 else k_swapped
+                    queries, c0 = q_mx[h // 2, c]
                     nc.tensor.matmul_mx(
                         out=banks[u][:, r, :],
                         lhsT=codes(keys, rows, r * P, P),
                         lhsT_scale=scales(keys, rows, r * P, P),
-                        rhs=codes(pl, rows, c0, QT),
-                        rhs_scale=scales(pl, rows, c0, QT),
+                        rhs=codes(queries, rows, c0, QT),
+                        rhs_scale=scales(queries, rows, c0, QT),
                         start=True,
                         stop=True,
                     )
 
         def cap(u):
-            capped[u] = work.tile([P, QT * PACK], F32, name="capped")
-            if u in early:
-                nc.scalar.activation(
-                    out=capped[u][:].rearrange("p (q r) -> p q r", r=PACK), in_=banks[u][:].rearrange("p r q -> p q r"), func=ACT.Tanh, scale=1.0 / CAP
-                )
-            else:
-                nc.scalar.activation(out=capped[u][:], in_=banks[u][:].rearrange("p r q -> p (r q)"), func=ACT.Tanh, scale=1.0 / CAP)
+            capped[u] = work.tile([P, PACK, QT], F32, name="capped")
+            nc.scalar.activation(out=capped[u][:], in_=banks[u][:], func=ACT.Tanh, scale=1.0 / CAP)
 
         def weigh(u):
             c = units[u][1]
-            scaled[u] = work.tile([P, QT * PACK], F32, name="scaled")
-            if u in early:
-                nc.vector.scalar_tensor_tensor(out=scaled[u][:], in0=capped[u][:], scalar=0.0, in1=woven[c][:], op0=ALU.max, op1=ALU.mult)
-            else:
-                nc.vector.scalar_tensor_tensor(
-                    out=scaled[u][:].rearrange("p (r q) -> p r q", r=PACK),
-                    in0=capped[u][:].rearrange("p (r q) -> p r q", r=PACK),
-                    scalar=0.0,
-                    in1=weight[:, :, c * QT : (c + 1) * QT],
-                    op0=ALU.max,
-                    op1=ALU.mult,
-                )
+            scaled[u] = work.tile([P, PACK, QT], F32, name="scaled")
+            nc.vector.scalar_tensor_tensor(
+                out=scaled[u][:], in0=capped[u][:], scalar=0.0, in1=weight[:, :, c * QT : (c + 1) * QT], op0=ALU.max, op1=ALU.mult
+            )
 
         def square(u):
             squared[u] = work.tile([P, QT * PACK], BF16, name="squared", align_bytes=64)
-            if u in on_vector:
-                nc.vector.tensor_tensor(out=squared[u][:], in0=scaled[u][:], in1=scaled[u][:], op=ALU.mult)
-            elif u in early:
-                nc.scalar.activation(out=squared[u][:], in_=scaled[u][:], func=ACT.Square)
-            else:
-                nc.scalar.activation(
-                    out=squared[u][:].rearrange("p (b i r) -> p b r i", i=RUN, r=PACK),
-                    in_=scaled[u][:].rearrange("p (r b i) -> p b r i", i=RUN, r=PACK),
-                    func=ACT.Square,
-                )
+            nc.scalar.activation(
+                out=squared[u][:].rearrange("p (b i r) -> p b r i", i=RUN, r=PACK),
+                in_=scaled[u][:].rearrange("p r (b i) -> p b r i", i=RUN),
+                func=ACT.Square,
+            )
 
         def quantize_w(u):
-            w_pl[u] = planes("w_pl%d" % u, QT)
-            quantize(w_pl[u], squared[u][:])
-
-        def slot(u):
-            return 2 * (units[u][0] % 2) + units[u][1] % 2
+            w_mx[u] = new_operand("w_mx%d" % u, QT)
+            quantize(w_mx[u], squared[u][:])
 
         def mix(u):
             g = [i for i, members in enumerate(groups) if u in members][0]
-            if g not in sums:
-                sums[g] = psum.tile([P, 4, E], F32, name="sums", bufs=4)
+            if u == groups[g].start:
+                sums[g] = psum.tile([P, len(groups[g]), E], F32, name="sums", bufs=SUM_BANKS)
             e0 = (units[u][0] // 2) * E
             nc.tensor.matmul_mx(
-                out=sums[g][:, slot(u), :],
-                lhsT=codes(w_pl[u], every, 0, QT),
-                lhsT_scale=scales(w_pl[u], every, 0, QT),
-                rhs=codes(v_pl, every, e0, E),
-                rhs_scale=scales(v_pl, every, e0, E),
+                out=sums[g][:, u - groups[g].start, :],
+                lhsT=codes(w_mx[u], every, 0, QT),
+                lhsT_scale=scales(w_mx[u], every, 0, QT),
+                rhs=codes(v_mx, every, e0, E),
+                rhs_scale=scales(v_mx, every, e0, E),
                 start=True,
                 stop=True,
             )
 
-        dens, recs = {}, {}
-
-        def span(g):
-            used = [slot(u) for u in groups[g]]
-            return slice(min(used), max(used) + 1)
-
         def denominators(g):
-            dens[g] = keep.tile([P, 4], F32, name="den%d" % g)
-            nc.vector.tensor_scalar(out=dens[g][:, span(g)], in0=sums[g][:, span(g), E - 1], scalar1=1.0, scalar2=None, op0=ALU.add)
+            dens[g] = keep.tile([P, len(groups[g])], F32, name="den%d" % g)
+            nc.vector.tensor_scalar(out=dens[g][:], in0=sums[g][:, :, E - 1], scalar1=1.0, scalar2=None, op0=ALU.add)
 
         def reciprocals(g):
-            recs[g] = keep.tile([P, 4], F32, name="rec%d" % g)
-            nc.vector.reciprocal(out=recs[g][:, span(g)], in_=dens[g][:, span(g)])
+            recs[g] = keep.tile([P, len(groups[g])], F32, name="rec%d" % g)
+            nc.vector.reciprocal(out=recs[g][:], in_=dens[g][:])
 
         def finish(g):
             for h in sorted(set(units[u][0] for u in groups[g])):
@@ -260,86 +228,83 @@ def tile_rows_a_relu2_mask_cap_gate_kernel(tc, qT, kT, t, v, mask, og, out):
                 c0 = units[members[0]][1]
                 res = keep.tile([P, len(members), E], F32, name="res%d%d" % (g, h))
                 for i, u in enumerate(members):
+                    place = u - groups[g].start
                     nc.vector.scalar_tensor_tensor(
                         out=res[:, i, :],
-                        in0=sums[g][:, slot(u), :],
-                        scalar=recs[g][:, slot(u) : slot(u) + 1],
+                        in0=sums[g][:, place, :],
+                        scalar=recs[g][:, place : place + 1],
                         in1=gate[:, h * TILES + c0 + i, :],
                         op0=ALU.mult,
                         op1=ALU.mult,
                     )
                 nc.sync.dma_start(out=out_rows[h][:, c0 : c0 + len(members), :], in_=res[:])
 
-        def gates_a(lo, hi):
-            nc.scalar.activation(out=gate[:, lo:hi, :], in_=og_a[:, lo - 1 : hi - 1, :], func=ACT.Sigmoid)
+        def gates(g):
+            if g < 2:
+                lo, hi = max(g * TILES, 1), (g + 1) * TILES
+                nc.scalar.activation(out=gate[:, lo:hi, :], in_=og_low[:, lo - 1 : hi - 1, :], func=ACT.Sigmoid)
+            else:
+                c0 = units[groups[g].start][1]
+                nc.scalar.activation(
+                    out=gate[:, 2 * TILES :, :].rearrange("p (h c) e -> p h c e", h=2)[:, :, c0 : c0 + 2, :],
+                    in_=og_high[:].rearrange("p (h c) e -> p h c e", h=2)[:, :, c0 : c0 + 2, :],
+                    func=ACT.Sigmoid,
+                )
 
-        def gates_b(c0):
-            nc.scalar.activation(
-                out=gate[:, 2 * TILES :, :].rearrange("p (h c) e -> p h c e", h=2)[:, :, c0 : c0 + 2, :],
-                in_=og_b[:].rearrange("p (h c) e -> p h c e", h=2)[:, :, c0 : c0 + 2, :],
-                func=ACT.Sigmoid,
-            )
-
-        on_vector = ()
-        extra = {
-            1: [lambda: scale_mask(1, 1)],
-            2: [lambda: scale_mask(2, 2)],
-            4: [lambda: interleave_q(1, 0, 2, vcopy)],
-            5: [lambda: quantize_q(1, 0), sign_v],
-            6: [interleave_v, lambda: gates_a(1, 4)],
-            7: [lambda: quantize(v_pl, v_bf[:]), lambda: interleave_q(1, 2, 2, vcopy), lambda: gates_a(4, 8)],
-            8: [lambda: quantize_q(1, 2)],
-            9: [lambda: denominators(0), lambda: gates_b(0)],
-            10: [lambda: reciprocals(0)],
-            11: [lambda: finish(0)],
-            12: [lambda: denominators(1)],
-            13: [lambda: reciprocals(1)],
-            14: [lambda: finish(1)],
-            16: [lambda: denominators(2)],
-            17: [lambda: reciprocals(2)],
-            18: [lambda: finish(2)],
-        }
-
-        def previous(u):
-            same = [x for x in range(u) if units[x][0] % 2 == units[u][0] % 2]
-            return same[-2] if len(same) >= 2 else -1
-
+        interleave_q(0, 0, 1, nc.vector.tensor_copy)
+        interleave_q(0, 1, 1, nc.scalar.copy)
+        quantize_q(0, 0)
         scores(blocks[0])
-        interleave_q(0, 2, 2, vcopy)
+        interleave_q(0, 2, 2, nc.vector.tensor_copy)
         quantize_q(0, 1)
         scores(blocks[1])
         quantize_q(0, 2)
         scale_mask(0, 1)
-        done = {"square": 0, "quantize": 0, "mix": 0, "block": 2}
-        for i in range(count + 3):
-            lag = 2 if i < 0 else 3
-            if done["square"] <= i - lag and done["square"] not in on_vector:
-                square(done["square"])
-                done["square"] = done["square"] + 1
-            if 0 <= i - 1 < count:
-                weigh(i - 1)
-            if i < count:
-                cap(i)
-            if done["quantize"] <= i - lag - 1:
-                quantize_w(done["quantize"])
-                done["quantize"] = done["quantize"] + 1
-            if done["square"] <= i - lag:
-                square(done["square"])
-                done["square"] = done["square"] + 1
-            for step in extra.get(i, []):
-                step()
-            while done["block"] < len(blocks) and max(previous(u) for u in blocks[done["block"]]) <= i:
-                scores(blocks[done["block"]])
-                done["block"] = done["block"] + 1
-            while i >= 8 and done["mix"] < done["quantize"]:
-                mix(done["mix"])
-                done["mix"] = done["mix"] + 1
-        gates_b(2)
-        quantize_w(count - 1)
-        mix(count - 1)
-        denominators(3)
-        reciprocals(3)
-        finish(3)
-        denominators(4)
-        reciprocals(4)
-        finish(4)
+        scale_mask(1, 1)
+
+        side = [
+            [lambda: interleave_q(1, 0, 2, nc.vector.tensor_copy)],
+            [lambda: quantize_q(1, 0), sign_v],
+            [interleave_v],
+            [lambda: quantize(v_mx, v_bf[:]), lambda: interleave_q(1, 2, 2, nc.vector.tensor_copy)],
+            [lambda: quantize_q(1, 2)],
+        ]
+        first_mix_step = FIRST_SIDE_STEP + len(side) - 1
+        den_step = [max(members.stop - 1 + SQUARE_LAG, first_mix_step) + 1 for members in groups]
+        last_step = count - 1 + SQUARE_LAG
+        gate_step = den_step[:3] + [last_step]
+        next_block, next_mix = 2, 0
+        for step in range(last_step + 1):
+            ready = [g for g in range(len(groups)) if den_step[g] == step]
+            if step >= SQUARE_LAG:
+                square(step - SQUARE_LAG)
+            if 1 <= step <= count:
+                weigh(step - 1)
+            if step < count:
+                cap(step)
+            for g in ready:
+                denominators(g)
+            if step >= SQUARE_LAG:
+                quantize_w(step - SQUARE_LAG)
+            if step == 2:
+                scale_mask(2, 2)
+            if 0 <= step - FIRST_SIDE_STEP < len(side):
+                for job in side[step - FIRST_SIDE_STEP]:
+                    job()
+            for g in range(len(gate_step)):
+                if step == gate_step[g]:
+                    gates(g)
+            for g in ready:
+                reciprocals(g)
+            for g in range(len(groups)):
+                if den_step[g] + 1 == step:
+                    finish(g)
+            while next_block < len(blocks) and blocks[next_block][0] <= step + AHEAD:
+                scores(blocks[next_block])
+                next_block = next_block + 1
+            while step >= first_mix_step and next_mix <= step - SQUARE_LAG:
+                mix(next_mix)
+                next_mix = next_mix + 1
+        denominators(len(groups) - 1)
+        reciprocals(len(groups) - 1)
+        finish(len(groups) - 1)

@@ -26,6 +26,7 @@ SUM_BANKS = 2
 AHEAD = 2
 SQUARE_LAG = 3
 WORK_BUFS = SQUARE_LAG + 2
+WOVEN_TILE = 2
 FIRST_SIDE_STEP = 4
 
 
@@ -39,6 +40,8 @@ def tile_rows_a_relu2_mask_cap_gate_kernel(tc, qT, kT, t, v, mask, og, out):
     count = len(units)
     half = count // 2
     blocks = [[u] for u in range(half)] + [[u, u + 1] for u in range(half, count, 2)]
+    woven_units = [units.index((h, WOVEN_TILE)) for h in (2, 3)]
+    vector_unit = woven_units[0]
     groups = [range(0, 4), range(4, 8), range(8, 12), range(12, 14), range(14, 16)]
 
     with ExitStack() as ctx:
@@ -135,6 +138,12 @@ def tile_rows_a_relu2_mask_cap_gate_kernel(tc, qT, kT, t, v, mask, og, out):
                     out=weight[:, r, cols], in0=mask_raw[:, r, cols], scalar1=root[:, r : r + 1], scalar2=None, op0=ALU.mult
                 )
 
+        woven_weight = keep.tile([P, QT, PACK], F32)
+
+        def weave_weight():
+            cols = slice(WOVEN_TILE * QT, (WOVEN_TILE + 1) * QT)
+            nc.vector.tensor_copy(out=woven_weight[:], in_=weight[:, :, cols].rearrange("p r q -> p q r"))
+
         v_signed = keep.tile([P, KV, PACK, E], F32)
         v_bf = keep.tile([P, KV * E * PACK], BF16, align_bytes=64)
         v_mx = new_operand("v_mx", KV * E)
@@ -177,23 +186,33 @@ def tile_rows_a_relu2_mask_cap_gate_kernel(tc, qT, kT, t, v, mask, og, out):
                     )
 
         def cap(u):
-            capped[u] = work.tile([P, PACK, QT], F32, name="capped")
-            nc.scalar.activation(out=capped[u][:], in_=banks[u][:], func=ACT.Tanh, scale=1.0 / CAP)
+            if u in woven_units:
+                capped[u] = work.tile([P, QT, PACK], F32, name="capped")
+                src = banks[u][:].rearrange("p r q -> p q r")
+            else:
+                capped[u] = work.tile([P, PACK, QT], F32, name="capped")
+                src = banks[u][:]
+            nc.scalar.activation(out=capped[u][:], in_=src, func=ACT.Tanh, scale=1.0 / CAP)
 
         def weigh(u):
             c = units[u][1]
-            scaled[u] = work.tile([P, PACK, QT], F32, name="scaled")
-            nc.vector.scalar_tensor_tensor(
-                out=scaled[u][:], in0=capped[u][:], scalar=0.0, in1=weight[:, :, c * QT : (c + 1) * QT], op0=ALU.max, op1=ALU.mult
-            )
+            factor = woven_weight[:] if u in woven_units else weight[:, :, c * QT : (c + 1) * QT]
+            scaled[u] = work.tile(list(capped[u].shape), F32, name="scaled")
+            nc.vector.scalar_tensor_tensor(out=scaled[u][:], in0=capped[u][:], scalar=0.0, in1=factor, op0=ALU.max, op1=ALU.mult)
 
         def square(u):
             squared[u] = work.tile([P, QT * PACK], BF16, name="squared", align_bytes=64)
-            nc.scalar.activation(
-                out=squared[u][:].rearrange("p (b i r) -> p b r i", i=RUN, r=PACK),
-                in_=scaled[u][:].rearrange("p r (b i) -> p b r i", i=RUN),
-                func=ACT.Square,
-            )
+            if u == vector_unit:
+                src = scaled[u][:].rearrange("p q r -> p (q r)")
+                nc.vector.tensor_tensor(out=squared[u][:], in0=src, in1=src, op=ALU.mult)
+            elif u in woven_units:
+                nc.scalar.activation(out=squared[u][:], in_=scaled[u][:].rearrange("p q r -> p (q r)"), func=ACT.Square)
+            else:
+                nc.scalar.activation(
+                    out=squared[u][:].rearrange("p (b i r) -> p b r i", i=RUN, r=PACK),
+                    in_=scaled[u][:].rearrange("p r (b i) -> p b r i", i=RUN),
+                    func=ACT.Square,
+                )
 
         def quantize_w(u):
             w_mx[u] = new_operand("w_mx%d" % u, QT)
@@ -276,7 +295,7 @@ def tile_rows_a_relu2_mask_cap_gate_kernel(tc, qT, kT, t, v, mask, og, out):
         next_block, next_mix = 2, 0
         for step in range(last_step + 1):
             ready = [g for g in range(len(groups)) if den_step[g] == step]
-            if step >= SQUARE_LAG:
+            if step >= SQUARE_LAG and step - SQUARE_LAG != vector_unit:
                 square(step - SQUARE_LAG)
             if 1 <= step <= count:
                 weigh(step - 1)
@@ -286,6 +305,10 @@ def tile_rows_a_relu2_mask_cap_gate_kernel(tc, qT, kT, t, v, mask, og, out):
                 denominators(g)
             if step >= SQUARE_LAG:
                 quantize_w(step - SQUARE_LAG)
+            if step == vector_unit:
+                weave_weight()
+            if step == vector_unit + SQUARE_LAG - 1:
+                square(vector_unit)
             if step == 2:
                 scale_mask(2, 2)
             if 0 <= step - FIRST_SIDE_STEP < len(side):

from contextlib import ExitStack

import concourse.mybir as mybir

H, KV, D, NQ, N, E = 4, 2, 256, 512, 512, 128
CAP = 2.0
FLOPS = 2 * H * NQ * N * (D + E)

F32 = mybir.dt.float32
BF16 = mybir.dt.bfloat16
I32 = mybir.dt.int32
U8 = mybir.dt.uint8
FP8X4 = mybir.dt.float8_e4m3fn_x4
ACT = mybir.ActivationFunctionType
ALU = mybir.AluOpType

P = 128
PACK = 4
ROWS = D // PACK
QT = 128
TILES = NQ // QT
RUN = 4
K_ON_VECTOR = 88
SCORE_BANKS = 3
SUM_BANKS = 2
AHEAD = 2
SQUARE_LAG = 3
WORK_BUFS = SQUARE_LAG + 2
WOVEN_TILE = 2
FIRST_SIDE_STEP = 4


def tile_rows_a_relu2_mask_cap_gate_kernel(tc, qT, kT, t, v, mask, og, out):
    nc = tc.nc
    q_rows = qT.rearrange("(g h) (p j) n -> g (h p) j n", h=2, j=PACK)
    og_rows = og.rearrange("h (c m) e -> m (h c) e", m=QT)
    out_rows = out.rearrange("h (c m) e -> h m c e", m=QT)

    units = [(h, c) for h in (0, 1) for c in range(TILES)] + [(h, c) for c in range(TILES) for h in (2, 3)]
    count = len(units)
    half = count // 2
    blocks = [[u] for u in range(half)] + [[u, u + 1] for u in range(half, count, 2)]
    woven_units = [units.index((h, WOVEN_TILE)) for h in (2, 3)]
    vector_unit = woven_units[0]
    groups = [range(0, 4), range(4, 8), range(8, 12), range(12, 14), range(14, 16)]

    with ExitStack() as ctx:
        keep = ctx.enter_context(tc.tile_pool(name="keep", bufs=1))
        work = ctx.enter_context(tc.tile_pool(name="work", bufs=WORK_BUFS))
        psum = ctx.enter_context(tc.psum_pool(name="psum", bufs=1))
        ctx.enter_context(tc.manual_schedule())

        def load(name, src, queue):
            dst = keep.tile(list(src.shape), F32, name=name)
            queue.dma_start(out=dst[:], in_=src)
            return dst

        def new_operand(name, width):
            return keep.tile([P, width + width // 4], I32, name=name, align_bytes=64)

        def codes(operand, rows, c0, n):
            return operand[rows, c0 : c0 + n].bitcast(FP8X4)

        def scales(operand, rows, c0, n):
            width = operand.shape[1] * 4 // 5
            return operand[rows, width + c0 // 4 : width + (c0 + n) // 4].bitcast(U8)

        every = slice(0, P)

        def quantize(operand, src):
            n = src.shape[1] // PACK
            nc.vector.quantize_mx(out=codes(operand, every, 0, n), scales=scales(operand, every, 0, n), in_=src)

        t_sb = load("t_sb", t.rearrange("(p j) o -> p (j o)", j=PACK), nc.scalar)
        og_first = load("og_first", og_rows[:, 0:1, :], nc.scalar)
        k_raw = load("k_raw", kT.rearrange("h (p j) n -> (h p) j n", j=PACK), nc.sync)
        q_raw = [load("q_raw0", q_rows[0], nc.sync)]
        mask_raw = load("mask_raw", mask.rearrange("(p j) n -> p j n", j=PACK), nc.sync)

        k_mx = new_operand("k_mx", N)
        k_swapped = new_operand("k_swapped", N)
        nc.vector.memset(k_mx[:, N : N + N // 4], 0)

        t_abs = keep.tile([P, PACK], F32)
        guess = keep.tile([P, PACK], F32)
        t_sign = keep.tile([P, PACK], F32)
        inverse = keep.tile([P, PACK], F32)
        quotient = keep.tile([P, PACK], F32)
        root = keep.tile([P, PACK], F32)
        gate = keep.tile([P, H * TILES, E], F32)
        nc.vector.scalar_tensor_tensor(out=t_abs[:], in0=t_sb[:], scalar=-1.0, in1=t_sb[:], op0=ALU.mult, op1=ALU.max)
        nc.scalar.activation(out=guess[:], in_=t_abs[:], func=ACT.Sqrt, scale=CAP * CAP)
        nc.scalar.activation(out=t_sign[:], in_=t_sb[:], func=ACT.Sign)
        nc.scalar.activation(out=gate[:, 0:1, :], in_=og_first[:], func=ACT.Sigmoid)
        nc.vector.reciprocal(out=inverse[:], in_=guess[:])
        nc.vector.scalar_tensor_tensor(
            out=quotient[:], in0=inverse[:], scalar=0.5 * CAP * CAP, in1=t_abs[:], op0=ALU.mult, op1=ALU.mult
        )
        nc.vector.scalar_tensor_tensor(out=root[:], in0=guess[:], scalar=0.5, in1=quotient[:], op0=ALU.mult, op1=ALU.add)

        k_bf = keep.tile([P, PACK, P, PACK], BF16, align_bytes=64)
        for lo, hi, copy in ((0, K_ON_VECTOR, nc.vector.tensor_copy), (K_ON_VECTOR, P, nc.scalar.copy)):
            copy(
                out=k_bf[:, :, lo:hi, :].rearrange("p r s j -> p s j r"),
                in_=k_raw[:, :, lo * PACK : hi * PACK].rearrange("p j (s r) -> p s j r", r=PACK),
            )
        quantize(k_mx, k_bf[:].rearrange("p r s j -> p (r s j)"))

        nc.sync.dma_start(out=k_swapped[ROWS:P, :], in_=k_mx[0:ROWS, :])
        q_raw.append(load("q_raw1", q_rows[1], nc.sync))
        v_raw = load("v_raw", v.rearrange("h (p j) e -> p h (j e)", j=PACK), nc.sync)
        nc.sync.dma_start(out=k_swapped[0:ROWS, :], in_=k_mx[ROWS:P, :])
        og_low = load("og_low", og_rows[:, 1 : 2 * TILES, :], nc.sync)
        og_high = load("og_high", og_rows[:, 2 * TILES :, :], nc.sync)

        q_bf, q_mx = {}, {}

        def interleave_q(g, c, n, copy):
            q_bf[g, c] = keep.tile([P, n * QT * PACK], BF16, name="q_bf%d%d" % (g, c), align_bytes=64)
            copy(
                out=q_bf[g, c][:].rearrange("p (b i j) -> p b j i", i=RUN, j=PACK),
                in_=q_raw[g][:, :, c * QT : (c + n) * QT].rearrange("p j (b i) -> p b j i", i=RUN),
            )

        def quantize_q(g, c):
            width = q_bf[g, c].shape[1] // PACK
            operand = new_operand("q_mx%d%d" % (g, c), width)
            quantize(operand, q_bf[g, c][:])
            for i in range(width // QT):
                q_mx[g, c + i] = (operand, i * QT)

        weight = keep.tile([P, PACK, NQ], F32)

        def scale_mask(c, n):
            cols = slice(c * QT, (c + n) * QT)
            for r in range(PACK):
                nc.vector.tensor_scalar(
                    out=weight[:, r, cols], in0=mask_raw[:, r, cols], scalar1=root[:, r : r + 1], scalar2=None, op0=ALU.mult
                )

        woven_weight = keep.tile([P, QT, PACK], F32)

        def weave_weight():
            cols = slice(WOVEN_TILE * QT, (WOVEN_TILE + 1) * QT)
            nc.vector.tensor_copy(out=woven_weight[:], in_=weight[:, :, cols].rearrange("p r q -> p q r"))

        v_signed = keep.tile([P, KV, PACK, E], F32)
        v_bf = keep.tile([P, KV * E * PACK], BF16, align_bytes=64)
        v_mx = new_operand("v_mx", KV * E)

        def sign_v():
            for r in range(PACK):
                nc.vector.tensor_scalar(
                    out=v_signed[:, :, r, :],
                    in0=v_raw[:, :, r * E : (r + 1) * E],
                    scalar1=t_sign[:, r : r + 1],
                    scalar2=None,
                    op0=ALU.mult,
                )

        def interleave_v():
            nc.vector.tensor_copy(
                out=v_bf[:].rearrange("p (g b i r) -> p g b r i", g=KV, i=RUN, r=PACK),
                in_=v_signed[:].rearrange("p g r (b i) -> p g b r i", i=RUN),
            )

        banks, capped, scaled, squared, w_mx, sums, dens, recs = {}, {}, {}, {}, {}, {}, {}, {}

        def scores(block):
            for u in block:
                banks[u] = psum.tile([P, PACK, QT], F32, name="scores%d" % (units[u][0] % 2), bufs=SCORE_BANKS)
            for r in range(PACK):
                for u in block:
                    h, c = units[u]
                    rows = slice(ROWS * (h % 2), ROWS * (h % 2 + 1))
                    keys = k_mx if h // 2 == h % 2 else k_swapped
                    queries, c0 = q_mx[h // 2, c]
                    nc.tensor.matmul_mx(
                        out=banks[u][:, r, :],
                        lhsT=codes(keys, rows, r * P, P),
                        lhsT_scale=scales(keys, rows, r * P, P),
                        rhs=codes(queries, rows, c0, QT),
                        rhs_scale=scales(queries, rows, c0, QT),
                        start=True,
                        stop=True,
                    )

        def cap(u):
            if u in woven_units:
                capped[u] = work.tile([P, QT, PACK], F32, name="capped")
                src = banks[u][:].rearrange("p r q -> p q r")
            else:
                capped[u] = work.tile([P, PACK, QT], F32, name="capped")
                src = banks[u][:]
            nc.scalar.activation(out=capped[u][:], in_=src, func=ACT.Tanh, scale=1.0 / CAP)

        def weigh(u):
            c = units[u][1]
            factor = woven_weight[:] if u in woven_units else weight[:, :, c * QT : (c + 1) * QT]
            scaled[u] = work.tile(list(capped[u].shape), F32, name="scaled")
            nc.vector.scalar_tensor_tensor(out=scaled[u][:], in0=capped[u][:], scalar=0.0, in1=factor, op0=ALU.max, op1=ALU.mult)

        def square(u):
            squared[u] = work.tile([P, QT * PACK], BF16, name="squared", align_bytes=64)
            if u == vector_unit:
                src = scaled[u][:].rearrange("p q r -> p (q r)")
                nc.vector.tensor_tensor(out=squared[u][:], in0=src, in1=src, op=ALU.mult)
            elif u in woven_units:
                nc.scalar.activation(out=squared[u][:], in_=scaled[u][:].rearrange("p q r -> p (q r)"), func=ACT.Square)
            else:
                nc.scalar.activation(
                    out=squared[u][:].rearrange("p (b i r) -> p b r i", i=RUN, r=PACK),
                    in_=scaled[u][:].rearrange("p r (b i) -> p b r i", i=RUN),
                    func=ACT.Square,
                )

        def quantize_w(u):
            w_mx[u] = new_operand("w_mx%d" % u, QT)
            quantize(w_mx[u], squared[u][:])

        def mix(u):
            g = [i for i, members in enumerate(groups) if u in members][0]
            if u == groups[g].start:
                sums[g] = psum.tile([P, len(groups[g]), E], F32, name="sums", bufs=SUM_BANKS)
            e0 = (units[u][0] // 2) * E
            nc.tensor.matmul_mx(
                out=sums[g][:, u - groups[g].start, :],
                lhsT=codes(w_mx[u], every, 0, QT),
                lhsT_scale=scales(w_mx[u], every, 0, QT),
                rhs=codes(v_mx, every, e0, E),
                rhs_scale=scales(v_mx, every, e0, E),
                start=True,
                stop=True,
            )

        def denominators(g):
            dens[g] = keep.tile([P, len(groups[g])], F32, name="den%d" % g)
            nc.vector.tensor_scalar(out=dens[g][:], in0=sums[g][:, :, E - 1], scalar1=1.0, scalar2=None, op0=ALU.add)

        def reciprocals(g):
            recs[g] = keep.tile([P, len(groups[g])], F32, name="rec%d" % g)
            nc.vector.reciprocal(out=recs[g][:], in_=dens[g][:])

        def finish(g):
            for h in sorted(set(units[u][0] for u in groups[g])):
                members = [u for u in groups[g] if units[u][0] == h]
                c0 = units[members[0]][1]
                res = keep.tile([P, len(members), E], F32, name="res%d%d" % (g, h))
                for i, u in enumerate(members):
                    place = u - groups[g].start
                    nc.vector.scalar_tensor_tensor(
                        out=res[:, i, :],
                        in0=sums[g][:, place, :],
                        scalar=recs[g][:, place : place + 1],
                        in1=gate[:, h * TILES + c0 + i, :],
                        op0=ALU.mult,
                        op1=ALU.mult,
                    )
                nc.sync.dma_start(out=out_rows[h][:, c0 : c0 + len(members), :], in_=res[:])

        def gates(g):
            if g < 2:
                lo, hi = max(g * TILES, 1), (g + 1) * TILES
                nc.scalar.activation(out=gate[:, lo:hi, :], in_=og_low[:, lo - 1 : hi - 1, :], func=ACT.Sigmoid)
            else:
                c0 = units[groups[g].start][1]
                nc.scalar.activation(
                    out=gate[:, 2 * TILES :, :].rearrange("p (h c) e -> p h c e", h=2)[:, :, c0 : c0 + 2, :],
                    in_=og_high[:].rearrange("p (h c) e -> p h c e", h=2)[:, :, c0 : c0 + 2, :],
                    func=ACT.Sigmoid,
                )

        interleave_q(0, 0, 1, nc.vector.tensor_copy)
        interleave_q(0, 1, 1, nc.scalar.copy)
        quantize_q(0, 0)
        scores(blocks[0])
        interleave_q(0, 2, 2, nc.vector.tensor_copy)
        quantize_q(0, 1)
        scores(blocks[1])
        quantize_q(0, 2)
        scale_mask(0, 1)
        scale_mask(1, 1)

        side = [
            [lambda: interleave_q(1, 0, 2, nc.vector.tensor_copy)],
            [lambda: quantize_q(1, 0), sign_v],
            [interleave_v],
            [lambda: quantize(v_mx, v_bf[:]), lambda: interleave_q(1, 2, 2, nc.vector.tensor_copy)],
            [lambda: quantize_q(1, 2)],
        ]
        first_mix_step = FIRST_SIDE_STEP + len(side) - 1
        den_step = [max(members.stop - 1 + SQUARE_LAG, first_mix_step) + 1 for members in groups]
        last_step = count - 1 + SQUARE_LAG
        gate_step = den_step[:3] + [last_step]
        next_block, next_mix = 2, 0
        for step in range(last_step + 1):
            ready = [g for g in range(len(groups)) if den_step[g] == step]
            if step >= SQUARE_LAG and step - SQUARE_LAG != vector_unit:
                square(step - SQUARE_LAG)
            if 1 <= step <= count:
                weigh(step - 1)
            if step < count:
                cap(step)
            for g in ready:
                denominators(g)
            if step >= SQUARE_LAG:
                quantize_w(step - SQUARE_LAG)
            if step == vector_unit:
                weave_weight()
            if step == vector_unit + SQUARE_LAG - 1:
                square(vector_unit)
            if step == 2:
                scale_mask(2, 2)
            if 0 <= step - FIRST_SIDE_STEP < len(side):
                for job in side[step - FIRST_SIDE_STEP]:
                    job()
            for g in range(len(gate_step)):
                if step == gate_step[g]:
                    gates(g)
            for g in ready:
                reciprocals(g)
            for g in range(len(groups)):
                if den_step[g] + 1 == step:
                    finish(g)
            while next_block < len(blocks) and blocks[next_block][0] <= step + AHEAD:
                scores(blocks[next_block])
                next_block = next_block + 1
            while step >= first_mix_step and next_mix <= step - SQUARE_LAG:
                mix(next_mix)
                next_mix = next_mix + 1
        denominators(len(groups) - 1)
        reciprocals(len(groups) - 1)
        finish(len(groups) - 1)
